import numpy as np
import ml_dtypes


def mxq(x, axis, fmt="e4m3"):
    dtype, down = {"e4m3": (ml_dtypes.float8_e4m3fn, 7), "e5m2": (ml_dtypes.float8_e5m2, 14)}[fmt]
    v = np.moveaxis(np.asarray(x, np.float32).astype(ml_dtypes.bfloat16).astype(np.float64), axis, -1)
    blocks = v.reshape(v.shape[:-1] + (-1, 32))
    amax = np.abs(blocks).max(-1, keepdims=True)
    byte = np.maximum(np.where(amax > 0, np.frexp(amax)[1] - 1 + 127, 0) - down, 1)
    scale = np.exp2(byte - 127.0)
    codes = (blocks / scale).astype(np.float32).astype(dtype).astype(np.float64)
    return np.moveaxis((codes * scale).reshape(v.shape), -1, axis)


WIDE = False


def mx_kscale(k):
    if not WIDE:
        return np.ones(k)
    levels = np.array([10, -10, 5, -5, 0])
    if k % 512:
        return np.exp2(np.random.permutation(np.resize(levels, k // 32))).repeat(32)
    a = np.empty((k // 512, 16))
    for p in range(k // 512):
        a[p, :8] = np.random.permutation(np.resize(levels, 8))
        for g in range(8):
            far = levels[np.abs(levels - a[p, g]) >= 10]
            a[p, g + 8] = far[np.random.randint(len(far))]
    return np.exp2(a.ravel()).repeat(32)


def f64(x):
    return np.asarray(x).astype(np.float64)


def striped(idx):
    return np.tile(idx.reshape(-1, 16).T, (8, 1)).astype(np.uint16)


def unstriped(offs):
    return offs[:16].T.reshape(-1).astype(np.int64)


def pack_weight(w):
    k, n = w.shape
    w = f64(np.asarray(w, np.float32).astype(ml_dtypes.bfloat16)).reshape(k // 32, 32, n)
    amax = np.abs(w).max(1)
    byte = np.clip(np.where(amax > 0, np.frexp(amax)[1] - 1 + 127 - 7, 1), 1, 254)
    scaled = (w * np.exp2(127.0 - byte)[:, None, :]).reshape(k, n).astype(np.float32)
    words = np.ascontiguousarray(scaled.reshape(k // 512, 128, 4, n).transpose(0, 1, 3, 2)).astype(ml_dtypes.float8_e4m3fn).view(np.uint8)
    return words, np.ascontiguousarray(byte.astype(np.uint8).reshape(k // 512, 16, n))


def unpack_weight(words, scales):
    g, p, n, _ = words.shape
    vals = np.ascontiguousarray(words).view(ml_dtypes.float8_e4m3fn).astype(np.float64) * np.repeat(np.exp2(scales.astype(np.float64) - 127.0), 8, axis=1)[..., None]
    return vals.transpose(0, 1, 3, 2).reshape(g * 512, n)


E2M1 = np.array([0.0, 0.5, 1.0, 1.5, 2.0, 3.0, 4.0, 6.0, -0.0, -0.5, -1.0, -1.5, -2.0, -3.0, -4.0, -6.0])


def pack_fp4(w):
    k, n = w.shape
    w = f64(np.asarray(w, np.float32).astype(ml_dtypes.bfloat16)).reshape(k // 32, 32, n)
    amax = np.abs(w).max(1)
    mant, ex = np.frexp(amax / 6.0)
    byte = np.clip(np.where(amax > 0, np.where(mant > 0.5, ex, ex - 1) + 127, 1), 1, 254)
    scaled = (w * np.exp2(127.0 - byte)[:, None, :]).reshape(k, n).astype(np.float32)
    c = np.ascontiguousarray(scaled.reshape(k // 512, 128, 4, n).transpose(0, 1, 3, 2)).astype(ml_dtypes.float4_e2m1fn).view(np.uint8) & 0xF
    words = (c[..., 0::2] | (c[..., 1::2] << 4)).reshape(k // 512, 128, 2 * n)
    return np.ascontiguousarray(words), np.ascontiguousarray(byte.astype(np.uint8).reshape(k // 512, 16, n))


def unpack_fp4(words, scales):
    g, _, n = scales.shape
    words = np.ascontiguousarray(words).reshape(g, 128, n, 2)
    nib = np.empty((g, 128, n, 4), np.uint8)
    nib[..., 0::2] = words & 0xF
    nib[..., 1::2] = words >> 4
    vals = E2M1[nib] * np.repeat(np.exp2(scales.astype(np.float64) - 127.0), 8, axis=1)[..., None]
    return vals.transpose(0, 1, 3, 2).reshape(g * 512, n)


def planes(y):
    n, m = y.shape
    v = y.astype(np.float32).astype(ml_dtypes.bfloat16).astype(np.float64).reshape(n // 32, 32, m)
    top = np.abs(v).max(1)
    byte = np.clip(np.where(top > 0, np.frexp(top)[1] - 1 + 127 - 7, 1), 1, 254)
    codes = (v * np.exp2(127.0 - byte)[:, None, :]).reshape(n, m).astype(np.float32).astype(ml_dtypes.float8_e4m3fn).view(np.uint8)
    words = codes.reshape(n // 512, 128, 4, m).transpose(0, 1, 3, 2)
    return np.ascontiguousarray(words), np.ascontiguousarray(byte.astype(np.uint8).reshape(n // 512, 16, m))


K, T, S, D, V, H, N = 512, 2048, 1024, 2, 512, 512, 512


def setup_inputs():
    n = np.random.standard_normal
    s = mx_kscale(K)[:, None]
    u = mx_kscale(H)
    packed_xT = pack_weight(n((K, T)) * s)
    packed_w2 = pack_fp4(n((K, N)) / np.sqrt(K) / s)
    packed_w3 = pack_fp4(n((H, N)) / np.sqrt(H) / u[:, None])
    return {
        "x_words": packed_xT[0],
        "x_scales": packed_xT[1],
        "w1": (n((K, H)) / np.sqrt(K) / s * u).astype(np.float32),
        "w2_words": packed_w2[0],
        "w2_scales": packed_w2[1],
        "w3_words": packed_w3[0],
        "w3_scales": packed_w3[1],
        "offs": striped(np.random.permutation(T)[:S]),
    }


def reference(x_words, x_scales, w1, w2_words, w2_scales, w3_words, w3_scales, offs):
    xq = unpack_weight(x_words, x_scales)[:, unstriped(offs)]
    h = mxq(f64(w1), 0, "e4m3").T @ xq
    sh = h.reshape(H, V, D).sum(axis=2)
    e = unpack_fp4(w2_words, w2_scales).T @ xq
    se = e.reshape(H, V, D).sum(axis=2)
    z = sh * se - ((h * e).reshape(H, V, D).sum(axis=2))
    out_0 = unpack_fp4(w3_words, w3_scales).T @ mxq(z, 0, "e4m3")
    return (out_0,) + planes(out_0)

@@ -1,0 +1,219 @@
+from contextlib import ExitStack
+
+import concourse.mybir as mybir
+
+K, T, S, V, H, N = 512, 2048, 1024, 512, 512, 512
+FLOPS = 2 * K * H * S * 2 + 2 * H * N * V
+
+F32 = mybir.dt.float32
+BF16 = mybir.dt.bfloat16
+I32 = mybir.dt.int32
+U32 = mybir.dt.uint32
+U16 = mybir.dt.uint16
+U8 = mybir.dt.uint8
+FP8X4 = mybir.dt.float8_e4m3fn_x4
+FP4X4 = mybir.dt.float4_e2m1fn_x4
+MULT = mybir.AluOpType.mult
+ADD = mybir.AluOpType.add
+
+P = 128
+PACK = 4
+QUADS = 4
+CHUNK = 128
+RECS = CHUNK // 2
+GATHER = 256
+BLOCK = 128
+HALF = H // 2
+
+
+def load_scale_rows(queue, plane, scales):
+    for q in range(QUADS):
+        queue.dma_start(out=plane[32 * q : 32 * q + 4, :].bitcast(I32), in_=scales[0, 4 * q : 4 * q + 4, :].bitcast(I32))
+
+
+def tile_picked_zfm_none_po_kernel(
+    tc, x_words, x_scales, w1, w2_words, w2_scales, w3_words, w3_scales, offs, out_0, out_1, out_2
+):
+    nc = tc.nc
+    with ExitStack() as ctx:
+        keep = ctx.enter_context(tc.tile_pool(name="keep", bufs=1))
+        ring = ctx.enter_context(tc.tile_pool(name="ring", bufs=2))
+        psum_e = ctx.enter_context(tc.psum_pool(name="psum_e", bufs=3))
+        psum_h = ctx.enter_context(tc.psum_pool(name="psum_h", bufs=3))
+        psum_y = ctx.enter_context(tc.psum_pool(name="psum_y", bufs=2))
+
+        offsets = keep.tile([P, S // 16], U16, name="offsets")
+        x_table = keep.tile([P, T], U32, name="x_table", align_bytes=64)
+        x_table_scales = keep.tile([P, T], U8, name="x_table_scales", align_bytes=64)
+        x_codes = keep.tile([P, S], U32, name="x_codes", align_bytes=64)
+        x_plane = keep.tile([P, S], U8, name="x_plane", align_bytes=64)
+        w2_raw = keep.tile([P, 2 * H], U8, name="w2_raw", align_bytes=64)
+        w3_raw = keep.tile([P, 2 * N], U8, name="w3_raw", align_bytes=64)
+        w2_raw_scales = keep.tile([P, H], U8, name="w2_raw_scales", align_bytes=64)
+        w3_raw_scales = keep.tile([P, N], U8, name="w3_raw_scales", align_bytes=64)
+        w2_codes = keep.tile([P, 2 * H], U8, name="w2_codes", align_bytes=64)
+        w3_codes = keep.tile([P, 2 * N], U8, name="w3_codes", align_bytes=64)
+        w2_plane = keep.tile([P, H], U8, name="w2_plane", align_bytes=64)
+        w3_plane = keep.tile([P, N], U8, name="w3_plane", align_bytes=64)
+        w1_raw = [keep.tile([P, PACK, HALF], F32, name=f"w1_raw{u}", align_bytes=64) for u in range(2)]
+        w1_bf = [keep.tile([P, PACK, HALF // PACK, PACK], BF16, name=f"w1_bf{u}", align_bytes=64) for u in range(2)]
+        w1_codes = keep.tile([P, H], U32, name="w1_codes", align_bytes=64)
+        w1_plane = keep.tile([P, H], U8, name="w1_plane", align_bytes=64)
+        y_codes = keep.tile([P, V], U32, name="y_codes", align_bytes=64)
+        y_plane = keep.tile([P, V], U8, name="y_plane", align_bytes=64)
+
+        nc.vector.memset(w2_raw_scales[:].bitcast(I32), 0)
+        nc.vector.memset(w3_raw_scales[:].bitcast(I32), 0)
+
+        for q in range(QUADS):
+            queue = nc.sync if q % 2 == 0 else nc.scalar
+            queue.dma_start(
+                out=x_table_scales[32 * q : 32 * q + 32, :].bitcast(I32),
+                in_=x_scales[0, 4 * q : 4 * q + 4, :].bitcast(I32).partition_broadcast(8),
+            )
+        nc.sync.dma_start(offsets[:], offs)
+        nc.sync.dma_start(out=x_table[:].bitcast(I32), in_=x_words[0].rearrange("p n t -> p (n t)").bitcast(I32))
+        nc.sync.dma_start(out=w2_raw[:].bitcast(I32), in_=w2_words[0].bitcast(I32))
+        load_scale_rows(nc.sync, w2_raw_scales, w2_scales)
+        w1_rows = w1.rearrange("(p j) c -> p j c", j=PACK)
+        for u in range(2):
+            nc.sync.dma_start(out=w1_raw[u][:], in_=w1_rows[:, :, u * HALF : (u + 1) * HALF])
+        nc.sync.dma_start(out=w3_raw[:].bitcast(I32), in_=w3_words[0].bitcast(I32))
+        load_scale_rows(nc.sync, w3_raw_scales, w3_scales)
+
+        def deal(codes, plane, raw, raw_scales):
+            nc.scalar.copy(
+                out=codes[:].bitcast(U16).rearrange("p (t m) -> p t m", t=PACK),
+                in_=raw[:].bitcast(U16).rearrange("p (m t) -> p t m", t=PACK),
+            )
+            nc.gpsimd.tensor_copy(
+                out=plane[:].rearrange("p (t m) -> p t m", t=PACK),
+                in_=raw_scales[:].rearrange("p (m t) -> p t m", t=PACK),
+            )
+
+        nc.vector.tensor_copy(x_plane[:], x_table_scales[:].indirect(offsets[:]))
+        deal(w2_codes, w2_plane, w2_raw, w2_raw_scales)
+        for g in range(S // GATHER):
+            nc.vector.tensor_copy(
+                x_codes[:, g * GATHER : (g + 1) * GATHER],
+                x_table[:].indirect(offsets[:, g * GATHER // 16 : (g + 1) * GATHER // 16]),
+            )
+
+        def product(bank, lhs_codes, lhs_plane, rhs_codes, rhs_plane):
+            for t in range(PACK):
+                nc.tensor.matmul_mx(
+                    out=bank[:, t, :],
+                    lhsT=lhs_codes(t),
+                    lhsT_scale=lhs_plane[:, t * P : (t + 1) * P],
+                    rhs=rhs_codes.bitcast(FP8X4),
+                    rhs_scale=rhs_plane,
+                    start=True,
+                    stop=True,
+                )
+
+        def w1_slice(t):
+            return w1_codes[:, t * P : (t + 1) * P].bitcast(FP8X4)
+
+        def w2_slice(t):
+            return w2_codes[:, 2 * t * P : 2 * (t + 1) * P].bitcast(FP4X4)
+
+        def w3_slice(t):
+            return w3_codes[:, 2 * t * P : 2 * (t + 1) * P].bitcast(FP4X4)
+
+        def round_w1(u, copy):
+            copy(
+                out=w1_bf[u][:].rearrange("p t m j -> p m j t"),
+                in_=w1_raw[u][:].rearrange("p j (m t) -> p m j t", t=PACK),
+            )
+
+        def quantize_w1(u):
+            m = HALF // PACK
+            for t in range(PACK):
+                cols = slice(t * P + u * m, t * P + (u + 1) * m)
+                nc.vector.quantize_mx(
+                    out=w1_codes[:, cols].bitcast(FP8X4),
+                    scales=w1_plane[:, cols],
+                    in_=w1_bf[u][:, t, :, :].rearrange("p m j -> p (m j)"),
+                )
+
+        e_sb = [keep.tile([P, 2, RECS, PACK], F32, name=f"e_sb{c}", align_bytes=64) for c in range(S // CHUNK)]
+
+        def make_e(c):
+            cols = slice(c * CHUNK, (c + 1) * CHUNK)
+            e_bank = psum_e.tile([P, PACK, CHUNK], F32, name="e_bank")
+            product(e_bank, w2_slice, w2_plane, x_codes[:, cols], x_plane[:, cols])
+            nc.scalar.copy(out=e_sb[c][:], in_=e_bank[:].rearrange("p t (v d) -> p d v t", d=2))
+
+        def cross(c, pairs):
+            cols = slice(c * CHUNK, (c + 1) * CHUNK)
+            h_bank = psum_h.tile([P, PACK, CHUNK], F32, name="h_bank")
+            product(h_bank, w1_slice, w1_plane, x_codes[:, cols], x_plane[:, cols])
+            recs = slice((c % 2) * RECS, (c % 2 + 1) * RECS)
+            nc.vector.tensor_tensor(
+                out=pairs[:, :, recs, :],
+                in0=h_bank[:].rearrange("p t (v d) -> p d v t", d=2),
+                in1=e_sb[c][:, ::-1, :, :],
+                op=MULT,
+            )
+
+        make_e(0)
+        make_e(1)
+        round_w1(0, nc.scalar.copy)
+        quantize_w1(0)
+        round_w1(1, nc.vector.tensor_copy)
+        make_e(2)
+        make_e(3)
+        quantize_w1(1)
+        deal(w3_codes, w3_plane, w3_raw, w3_raw_scales)
+
+        out_rows = out_0.rearrange("(p t) v -> p t v", t=PACK)
+        out_words = out_1[0].rearrange("p v t -> p (v t)").bitcast(I32)
+        blocks = V // BLOCK
+        z_bf = {}
+        y_bf = {}
+
+        def last_product(b):
+            z_codes = ring.tile([P, BLOCK], U32, name="z_codes", align_bytes=64)
+            z_plane = ring.tile([P, BLOCK], U8, name="z_plane", align_bytes=64)
+            nc.vector.quantize_mx(out=z_codes[:].bitcast(FP8X4), scales=z_plane[:], in_=z_bf[b][:])
+            y_bank = psum_y.tile([P, PACK, BLOCK], F32, name="y_bank")
+            product(y_bank, w3_slice, w3_plane, z_codes[:], z_plane[:])
+            y_bf[b] = ring.tile([P, BLOCK, PACK], BF16, name="y_bf", align_bytes=64)
+            nc.scalar.copy(out=y_bf[b][:], in_=y_bank[:].rearrange("p t v -> p v t"))
+            y_sb = ring.tile([P, PACK, BLOCK], F32, name="y_sb", align_bytes=64)
+            nc.scalar.copy(out=y_sb[:], in_=y_bank[:])
+            nc.sync.dma_start(out=out_rows[:, :, b * BLOCK : (b + 1) * BLOCK], in_=y_sb[:])
+
+        def hand_on(b):
+            cols = slice(b * BLOCK, (b + 1) * BLOCK)
+            nc.vector.quantize_mx(
+                out=y_codes[:, cols].bitcast(FP8X4),
+                scales=y_plane[:, cols],
+                in_=y_bf[b][:].rearrange("p v t -> p (v t)"),
+            )
+            nc.sync.dma_start(out=out_words[:, cols], in_=y_codes[:, cols].bitcast(I32))
+
+        for b in range(blocks):
+            pairs = ring.tile([P, 2, BLOCK, PACK], F32, name="pairs", align_bytes=64)
+            cross(2 * b, pairs)
+            if b > 0:
+                last_product(b - 1)
+            if 2 * b + 4 < S // CHUNK:
+                make_e(2 * b + 4)
+                make_e(2 * b + 5)
+            cross(2 * b + 1, pairs)
+            if b > 1:
+                hand_on(b - 2)
+            z_bf[b] = ring.tile([P, BLOCK * PACK], BF16, name="z_bf", align_bytes=64)
+            nc.vector.tensor_tensor(
+                out=z_bf[b][:],
+                in0=pairs[:, 0, :, :].rearrange("p v t -> p (v t)"),
+                in1=pairs[:, 1, :, :].rearrange("p v t -> p (v t)"),
+                op=ADD,
+            )
+        hand_on(blocks - 2)
+        last_product(blocks - 1)
+        hand_on(blocks - 1)
+        for q in range(QUADS):
+            queue = nc.sync if q % 2 == 0 else nc.scalar
+            queue.dma_start(out=out_2[0, 4 * q : 4 * q + 4, :].bitcast(I32), in_=y_plane[32 * q : 32 * q + 4, :].bitcast(I32))

@@ -37,7 +37,7 @@ def tile_picked_zfm_none_po_kernel(
     nc = tc.nc
     with ExitStack() as ctx:
         keep = ctx.enter_context(tc.tile_pool(name="keep", bufs=1))
-        ring = ctx.enter_context(tc.tile_pool(name="ring", bufs=2))
+        ring = ctx.enter_context(tc.tile_pool(name="ring", bufs=4))
         psum_e = ctx.enter_context(tc.psum_pool(name="psum_e", bufs=3))
         psum_h = ctx.enter_context(tc.psum_pool(name="psum_h", bufs=3))
         psum_y = ctx.enter_context(tc.psum_pool(name="psum_y", bufs=2))
@@ -45,18 +45,16 @@ def tile_picked_zfm_none_po_kernel(
         offsets = keep.tile([P, S // 16], U16, name="offsets")
         x_table = keep.tile([P, T], U32, name="x_table", align_bytes=64)
         x_table_scales = keep.tile([P, T], U8, name="x_table_scales", align_bytes=64)
-        x_codes = keep.tile([P, S], U32, name="x_codes", align_bytes=64)
         x_plane = keep.tile([P, S], U8, name="x_plane", align_bytes=64)
         w2_raw = keep.tile([P, 2 * H], U8, name="w2_raw", align_bytes=64)
         w3_raw = keep.tile([P, 2 * N], U8, name="w3_raw", align_bytes=64)
-        w2_raw_scales = keep.tile([P, H], U8, name="w2_raw_scales", align_bytes=64)
+        w2_raw_scales = keep.tile([P, H], U8, name="w2_raw_scales", tag="w2_raw_scales", align_bytes=64)
         w3_raw_scales = keep.tile([P, N], U8, name="w3_raw_scales", align_bytes=64)
         w2_codes = keep.tile([P, 2 * H], U8, name="w2_codes", align_bytes=64)
         w3_codes = keep.tile([P, 2 * N], U8, name="w3_codes", align_bytes=64)
         w2_plane = keep.tile([P, H], U8, name="w2_plane", align_bytes=64)
-        w3_plane = keep.tile([P, N], U8, name="w3_plane", align_bytes=64)
-        w1_raw = [keep.tile([P, PACK, HALF], F32, name=f"w1_raw{u}", align_bytes=64) for u in range(2)]
-        w1_bf = [keep.tile([P, PACK, HALF // PACK, PACK], BF16, name=f"w1_bf{u}", align_bytes=64) for u in range(2)]
+        w1_raw = [keep.tile([P, PACK, HALF], F32, name=f"w1_raw{u}", tag=f"w1_raw{u}", align_bytes=64) for u in range(2)]
+        w1_bf = [keep.tile([P, PACK, HALF // PACK, PACK], BF16, name=f"w1_bf{u}", tag=f"w1_bf{u}", align_bytes=64) for u in range(2)]
         w1_codes = keep.tile([P, H], U32, name="w1_codes", align_bytes=64)
         w1_plane = keep.tile([P, H], U8, name="w1_plane", align_bytes=64)
         y_codes = keep.tile([P, V], U32, name="y_codes", align_bytes=64)
@@ -86,18 +84,24 @@ def tile_picked_zfm_none_po_kernel(
                 out=codes[:].bitcast(U16).rearrange("p (t m) -> p t m", t=PACK),
                 in_=raw[:].bitcast(U16).rearrange("p (m t) -> p t m", t=PACK),
             )
-            nc.gpsimd.tensor_copy(
+            nc.vector.tensor_copy(
                 out=plane[:].rearrange("p (t m) -> p t m", t=PACK),
                 in_=raw_scales[:].rearrange("p (m t) -> p t m", t=PACK),
             )
 
         nc.vector.tensor_copy(x_plane[:], x_table_scales[:].indirect(offsets[:]))
         deal(w2_codes, w2_plane, w2_raw, w2_raw_scales)
-        for g in range(S // GATHER):
-            nc.vector.tensor_copy(
-                x_codes[:, g * GATHER : (g + 1) * GATHER],
-                x_table[:].indirect(offsets[:, g * GATHER // 16 : (g + 1) * GATHER // 16]),
-            )
+        x_parts = {}
+
+        def gather_words(g, codes):
+            x_parts[g] = codes
+            nc.vector.tensor_copy(codes, x_table[:].indirect(offsets[:, g * GATHER // 16 : (g + 1) * GATHER // 16]))
+
+        x_first = keep.tile([P, GATHER], U32, name="x_first", align_bytes=64)
+        gather_words(0, x_first[:])
+        x_middle = keep.tile([P, 2 * GATHER], U32, name="x_middle", tag="w2_raw_scales", align_bytes=64)
+        gather_words(1, x_middle[:, :GATHER])
+        gather_words(2, x_middle[:, GATHER:])
 
         def product(bank, lhs_codes, lhs_plane, rhs_codes, rhs_plane):
             for t in range(PACK):
@@ -136,34 +140,47 @@ def tile_picked_zfm_none_po_kernel(
                     in_=w1_bf[u][:, t, :, :].rearrange("p m j -> p (m j)"),
                 )
 
-        e_sb = [keep.tile([P, 2, RECS, PACK], F32, name=f"e_sb{c}", align_bytes=64) for c in range(S // CHUNK)]
+        e_sb = {}
 
         def make_e(c):
             cols = slice(c * CHUNK, (c + 1) * CHUNK)
             e_bank = psum_e.tile([P, PACK, CHUNK], F32, name="e_bank")
-            product(e_bank, w2_slice, w2_plane, x_codes[:, cols], x_plane[:, cols])
-            nc.scalar.copy(out=e_sb[c][:], in_=e_bank[:].rearrange("p t (v d) -> p d v t", d=2))
+            product(e_bank, w2_slice, w2_plane, x_parts[c // 2][:, (c % 2) * CHUNK : (c % 2 + 1) * CHUNK], x_plane[:, cols])
+            if c % 4 == 0:
+                tag = "w1_raw0" if c == 0 else "e_late"
+                e_sb[c // 4] = keep.tile([P, 4, 2, RECS, PACK], F32, name=f"e_sb{c // 4}", tag=tag, align_bytes=64)
+            nc.scalar.copy(out=e_sb[c // 4][:, c % 4, :, :, :], in_=e_bank[:].rearrange("p t (v d) -> p d v t", d=2))
 
-        def cross(c, pairs):
+        def cross(c):
             cols = slice(c * CHUNK, (c + 1) * CHUNK)
             h_bank = psum_h.tile([P, PACK, CHUNK], F32, name="h_bank")
-            product(h_bank, w1_slice, w1_plane, x_codes[:, cols], x_plane[:, cols])
-            recs = slice((c % 2) * RECS, (c % 2 + 1) * RECS)
+            product(h_bank, w1_slice, w1_plane, x_parts[c // 2][:, (c % 2) * CHUNK : (c % 2 + 1) * CHUNK], x_plane[:, cols])
+            pairs = ring.tile([P, 2, RECS, PACK], F32, name="pairs", align_bytes=64)
             nc.vector.tensor_tensor(
-                out=pairs[:, :, recs, :],
+                out=pairs[:],
                 in0=h_bank[:].rearrange("p t (v d) -> p d v t", d=2),
-                in1=e_sb[c][:, ::-1, :, :],
+                in1=e_sb[c // 4][:, c % 4, ::-1, :, :],
                 op=MULT,
             )
+            if c % 2 == 0:
+                z_bf[c // 2] = ring.tile([P, BLOCK * PACK], BF16, name="z_bf", align_bytes=64)
+            adder = nc.vector if c == S // CHUNK - 1 else nc.gpsimd
+            adder.tensor_tensor(
+                out=z_bf[c // 2][:, (c % 2) * RECS * PACK : (c % 2 + 1) * RECS * PACK],
+                in0=pairs[:, 0, :, :].rearrange("p v t -> p (v t)"),
+                in1=pairs[:, 1, :, :].rearrange("p v t -> p (v t)"),
+                op=ADD,
+            )
 
-        make_e(0)
-        make_e(1)
         round_w1(0, nc.scalar.copy)
         quantize_w1(0)
         round_w1(1, nc.vector.tensor_copy)
-        make_e(2)
-        make_e(3)
+        x_last = keep.tile([P, GATHER], U32, name="x_last", tag="w1_raw1", align_bytes=64)
+        gather_words(3, x_last[:])
         quantize_w1(1)
+        for c in range(4):
+            make_e(c)
+        w3_plane = keep.tile([P, N], U8, name="w3_plane", tag="w1_bf1", align_bytes=64)
         deal(w3_codes, w3_plane, w3_raw, w3_raw_scales)
 
         out_rows = out_0.rearrange("(p t) v -> p t v", t=PACK)
@@ -182,7 +199,8 @@ def tile_picked_zfm_none_po_kernel(
             nc.scalar.copy(out=y_bf[b][:], in_=y_bank[:].rearrange("p t v -> p v t"))
             y_sb = ring.tile([P, PACK, BLOCK], F32, name="y_sb", align_bytes=64)
             nc.scalar.copy(out=y_sb[:], in_=y_bank[:])
-            nc.sync.dma_start(out=out_rows[:, :, b * BLOCK : (b + 1) * BLOCK], in_=y_sb[:])
+            queue = nc.scalar if b == blocks - 1 else nc.sync
+            queue.dma_start(out=out_rows[:, :, b * BLOCK : (b + 1) * BLOCK], in_=y_sb[:])
 
         def hand_on(b):
             cols = slice(b * BLOCK, (b + 1) * BLOCK)
@@ -193,27 +211,18 @@ def tile_picked_zfm_none_po_kernel(
             )
             nc.sync.dma_start(out=out_words[:, cols], in_=y_codes[:, cols].bitcast(I32))
 
+        cross(0)
         for b in range(blocks):
-            pairs = ring.tile([P, 2, BLOCK, PACK], F32, name="pairs", align_bytes=64)
-            cross(2 * b, pairs)
-            if b > 0:
-                last_product(b - 1)
+            cross(2 * b + 1)
             if 2 * b + 4 < S // CHUNK:
                 make_e(2 * b + 4)
                 make_e(2 * b + 5)
-            cross(2 * b + 1, pairs)
-            if b > 1:
-                hand_on(b - 2)
-            z_bf[b] = ring.tile([P, BLOCK * PACK], BF16, name="z_bf", align_bytes=64)
-            nc.vector.tensor_tensor(
-                out=z_bf[b][:],
-                in0=pairs[:, 0, :, :].rearrange("p v t -> p (v t)"),
-                in1=pairs[:, 1, :, :].rearrange("p v t -> p (v t)"),
-                op=ADD,
-            )
-        hand_on(blocks - 2)
-        last_product(blocks - 1)
+            if b < blocks - 1:
+                cross(2 * b + 2)
+            if b > 0:
+                hand_on(b - 1)
+            last_product(b)
         hand_on(blocks - 1)
         for q in range(QUADS):
-            queue = nc.sync if q % 2 == 0 else nc.scalar
+            queue = nc.scalar if q == QUADS - 1 else nc.sync
             queue.dma_start(out=out_2[0, 4 * q : 4 * q + 4, :].bitcast(I32), in_=y_plane[32 * q : 32 * q + 4, :].bitcast(I32))

@@ -54,7 +54,7 @@ def tile_picked_zfm_none_po_kernel(
         w3_codes = keep.tile([P, 2 * N], U8, name="w3_codes", align_bytes=64)
         w2_plane = keep.tile([P, H], U8, name="w2_plane", align_bytes=64)
         w1_raw = [keep.tile([P, PACK, HALF], F32, name=f"w1_raw{u}", tag=f"w1_raw{u}", align_bytes=64) for u in range(2)]
-        w1_bf = [keep.tile([P, PACK, HALF // PACK, PACK], BF16, name=f"w1_bf{u}", tag=f"w1_bf{u}", align_bytes=64) for u in range(2)]
+        w1_bf = {s: keep.tile([P, 2, P, PACK], BF16, name=f"w1_bf{s}", tag=f"w1_bf{s}", align_bytes=64) for s in (0, 2)}
         w1_codes = keep.tile([P, H], U32, name="w1_codes", align_bytes=64)
         w1_plane = keep.tile([P, H], U8, name="w1_plane", align_bytes=64)
         y_codes = keep.tile([P, V], U32, name="y_codes", align_bytes=64)
@@ -99,12 +99,13 @@ def tile_picked_zfm_none_po_kernel(
 
         x_first = keep.tile([P, GATHER], U32, name="x_first", align_bytes=64)
         gather_words(0, x_first[:])
-        x_middle = keep.tile([P, 2 * GATHER], U32, name="x_middle", tag="w2_raw_scales", align_bytes=64)
-        gather_words(1, x_middle[:, :GATHER])
-        gather_words(2, x_middle[:, GATHER:])
+        x_rest = keep.tile([P, S - GATHER], U32, name="x_rest", tag="w2_raw_scales", align_bytes=64)
+        nc.vector.tensor_copy(x_rest[:], x_table[:].indirect(offsets[:, GATHER // 16 :]))
+        for g in range(1, S // GATHER):
+            x_parts[g] = x_rest[:, (g - 1) * GATHER : g * GATHER]
 
-        def product(bank, lhs_codes, lhs_plane, rhs_codes, rhs_plane):
-            for t in range(PACK):
+        def product(bank, lhs_codes, lhs_plane, rhs_codes, rhs_plane, slices=range(PACK)):
+            for t in slices:
                 nc.tensor.matmul_mx(
                     out=bank[:, t, :],
                     lhsT=lhs_codes(t),
@@ -124,21 +125,20 @@ def tile_picked_zfm_none_po_kernel(
         def w3_slice(t):
             return w3_codes[:, 2 * t * P : 2 * (t + 1) * P].bitcast(FP4X4)
 
-        def round_w1(u, copy):
+        def round_w1(u, s, copy):
+            m = HALF // PACK
             copy(
-                out=w1_bf[u][:].rearrange("p t m j -> p m j t"),
-                in_=w1_raw[u][:].rearrange("p j (m t) -> p m j t", t=PACK),
+                out=w1_bf[s][:, :, u * m : (u + 1) * m, :].rearrange("p t m j -> p m j t"),
+                in_=w1_raw[u][:].rearrange("p j (m t) -> p m j t", t=PACK)[:, :, :, s : s + 2],
             )
 
-        def quantize_w1(u):
-            m = HALF // PACK
-            for t in range(PACK):
-                cols = slice(t * P + u * m, t * P + (u + 1) * m)
-                nc.vector.quantize_mx(
-                    out=w1_codes[:, cols].bitcast(FP8X4),
-                    scales=w1_plane[:, cols],
-                    in_=w1_bf[u][:, t, :, :].rearrange("p m j -> p (m j)"),
-                )
+        def quantize_w1(s):
+            cols = slice(s * P, (s + 2) * P)
+            nc.vector.quantize_mx(
+                out=w1_codes[:, cols].bitcast(FP8X4),
+                scales=w1_plane[:, cols],
+                in_=w1_bf[s][:].rearrange("p t m j -> p (t m j)"),
+            )
 
         e_sb = {}
 
@@ -147,82 +147,113 @@ def tile_picked_zfm_none_po_kernel(
             e_bank = psum_e.tile([P, PACK, CHUNK], F32, name="e_bank")
             product(e_bank, w2_slice, w2_plane, x_parts[c // 2][:, (c % 2) * CHUNK : (c % 2 + 1) * CHUNK], x_plane[:, cols])
             if c % 4 == 0:
-                tag = "w1_raw0" if c == 0 else "e_late"
+                tag = "w1_raw1" if c == 0 else "e_late"
                 e_sb[c // 4] = keep.tile([P, 4, 2, RECS, PACK], F32, name=f"e_sb{c // 4}", tag=tag, align_bytes=64)
             nc.scalar.copy(out=e_sb[c // 4][:, c % 4, :, :, :], in_=e_bank[:].rearrange("p t (v d) -> p d v t", d=2))
 
-        def cross(c):
+        def cross(c, pairs):
             cols = slice(c * CHUNK, (c + 1) * CHUNK)
             h_bank = psum_h.tile([P, PACK, CHUNK], F32, name="h_bank")
             product(h_bank, w1_slice, w1_plane, x_parts[c // 2][:, (c % 2) * CHUNK : (c % 2 + 1) * CHUNK], x_plane[:, cols])
-            pairs = ring.tile([P, 2, RECS, PACK], F32, name="pairs", align_bytes=64)
+            recs = slice((c % 2) * RECS, (c % 2 + 1) * RECS)
             nc.vector.tensor_tensor(
-                out=pairs[:],
+                out=pairs[:, :, recs, :],
                 in0=h_bank[:].rearrange("p t (v d) -> p d v t", d=2),
                 in1=e_sb[c // 4][:, c % 4, ::-1, :, :],
                 op=MULT,
             )
-            if c % 2 == 0:
-                z_bf[c // 2] = ring.tile([P, BLOCK * PACK], BF16, name="z_bf", align_bytes=64)
-            adder = nc.vector if c == S // CHUNK - 1 else nc.gpsimd
-            adder.tensor_tensor(
-                out=z_bf[c // 2][:, (c % 2) * RECS * PACK : (c % 2 + 1) * RECS * PACK],
-                in0=pairs[:, 0, :, :].rearrange("p v t -> p (v t)"),
-                in1=pairs[:, 1, :, :].rearrange("p v t -> p (v t)"),
-                op=ADD,
-            )
 
-        round_w1(0, nc.scalar.copy)
+        round_w1(0, 0, nc.scalar.copy)
+        round_w1(0, 2, nc.scalar.copy)
+        round_w1(1, 0, nc.scalar.copy)
+        round_w1(1, 2, nc.scalar.copy)
         quantize_w1(0)
-        round_w1(1, nc.vector.tensor_copy)
-        x_last = keep.tile([P, GATHER], U32, name="x_last", tag="w1_raw1", align_bytes=64)
-        gather_words(3, x_last[:])
-        quantize_w1(1)
+        quantize_w1(2)
         for c in range(4):
             make_e(c)
-        w3_plane = keep.tile([P, N], U8, name="w3_plane", tag="w1_bf1", align_bytes=64)
+        w3_plane = keep.tile([P, N], U8, name="w3_plane", tag="w1_bf2", align_bytes=64)
         deal(w3_codes, w3_plane, w3_raw, w3_raw_scales)
 
         out_rows = out_0.rearrange("(p t) v -> p t v", t=PACK)
         out_words = out_1[0].rearrange("p v t -> p (v t)").bitcast(I32)
         blocks = V // BLOCK
         z_bf = {}
-        y_bf = {}
+        y_early = keep.tile([P, V - BLOCK, PACK], BF16, name="y_early", align_bytes=64)
+        y_late = keep.tile([P, BLOCK, PACK], BF16, name="y_late", align_bytes=64)
+
+        z_codes = keep.tile([P, V], U32, name="z_codes", align_bytes=64)
+        z_plane = keep.tile([P, V], U8, name="z_plane", align_bytes=64)
+
+        def sum_pairs(b, pairs, recs):
+            nc.vector.tensor_tensor(
+                out=z_bf[b][:, recs, :], in0=pairs[:, 0, recs, :], in1=pairs[:, 1, recs, :], op=ADD
+            )
+
+        def quantize_z(b, recs):
+            cols = slice(b * BLOCK + recs.start, b * BLOCK + recs.stop)
+            nc.vector.quantize_mx(
+                out=z_codes[:, cols].bitcast(FP8X4),
+                scales=z_plane[:, cols],
+                in_=z_bf[b][:, recs, :].rearrange("p v t -> p (v t)"),
+            )
 
         def last_product(b):
-            z_codes = ring.tile([P, BLOCK], U32, name="z_codes", align_bytes=64)
-            z_plane = ring.tile([P, BLOCK], U8, name="z_plane", align_bytes=64)
-            nc.vector.quantize_mx(out=z_codes[:].bitcast(FP8X4), scales=z_plane[:], in_=z_bf[b][:])
+            cols = slice(b * BLOCK, (b + 1) * BLOCK)
             y_bank = psum_y.tile([P, PACK, BLOCK], F32, name="y_bank")
-            product(y_bank, w3_slice, w3_plane, z_codes[:], z_plane[:])
-            y_bf[b] = ring.tile([P, BLOCK, PACK], BF16, name="y_bf", align_bytes=64)
-            nc.scalar.copy(out=y_bf[b][:], in_=y_bank[:].rearrange("p t v -> p v t"))
+            product(y_bank, w3_slice, w3_plane, z_codes[:, cols], z_plane[:, cols])
+            nc.scalar.copy(out=y_early[:, cols, :], in_=y_bank[:].rearrange("p t v -> p v t"))
             y_sb = ring.tile([P, PACK, BLOCK], F32, name="y_sb", align_bytes=64)
             nc.scalar.copy(out=y_sb[:], in_=y_bank[:])
-            queue = nc.scalar if b == blocks - 1 else nc.sync
-            queue.dma_start(out=out_rows[:, :, b * BLOCK : (b + 1) * BLOCK], in_=y_sb[:])
+            nc.sync.dma_start(out=out_rows[:, :, cols], in_=y_sb[:])
 
-        def hand_on(b):
+        def last_product_in_two_banks(b):
             cols = slice(b * BLOCK, (b + 1) * BLOCK)
+            banks = []
+            for s, copy in ((0, nc.scalar.copy), (2, nc.vector.tensor_copy)):
+                y_bank = psum_y.tile([P, PACK, BLOCK], F32, name="y_bank")
+                banks.append(y_bank)
+                product(y_bank, w3_slice, w3_plane, z_codes[:, cols], z_plane[:, cols], range(s, s + 2))
+                copy(out=y_late[:, :, s : s + 2], in_=y_bank[:, s : s + 2, :].rearrange("p t v -> p v t"))
+            for s in (0, 2):
+                y_sb = ring.tile([P, 2, BLOCK], F32, name="y_sb", align_bytes=64)
+                nc.scalar.copy(out=y_sb[:], in_=banks[s // 2][:, s : s + 2, :])
+                nc.scalar.dma_start(out=out_rows[:, s : s + 2, cols], in_=y_sb[:])
+
+        def hand_on(y_bf, cols):
             nc.vector.quantize_mx(
                 out=y_codes[:, cols].bitcast(FP8X4),
                 scales=y_plane[:, cols],
-                in_=y_bf[b][:].rearrange("p v t -> p (v t)"),
+                in_=y_bf[:].rearrange("p v t -> p (v t)"),
             )
             nc.sync.dma_start(out=out_words[:, cols], in_=y_codes[:, cols].bitcast(I32))
 
-        cross(0)
+        whole, first, second = slice(0, BLOCK), slice(0, RECS), slice(RECS, BLOCK)
+        pairs = [ring.tile([P, 2, BLOCK, PACK], F32, name="pairs", align_bytes=64) for b in range(blocks)]
         for b in range(blocks):
-            cross(2 * b + 1)
+            z_bf[b] = ring.tile([P, BLOCK, PACK], BF16, name="z_bf", align_bytes=64)
+        last = blocks - 1
+        cross(0, pairs[0])
+        cross(1, pairs[0])
+        for b in range(last):
             if 2 * b + 4 < S // CHUNK:
                 make_e(2 * b + 4)
                 make_e(2 * b + 5)
-            if b < blocks - 1:
-                cross(2 * b + 2)
-            if b > 0:
-                hand_on(b - 1)
-            last_product(b)
-        hand_on(blocks - 1)
+            cross(2 * b + 2, pairs[b + 1])
+            sum_pairs(b, pairs[b], whole)
+            if b + 1 == last:
+                sum_pairs(last, pairs[last], first)
+                quantize_z(b, whole)
+                last_product(b)
+                cross(2 * b + 3, pairs[b + 1])
+            else:
+                cross(2 * b + 3, pairs[b + 1])
+                quantize_z(b, whole)
+                last_product(b)
+        quantize_z(last, first)
+        sum_pairs(last, pairs[last], second)
+        quantize_z(blocks - 1, second)
+        hand_on(y_early, slice(0, V - BLOCK))
+        last_product_in_two_banks(blocks - 1)
+        hand_on(y_late, slice(V - BLOCK, V))
         for q in range(QUADS):
-            queue = nc.scalar if q == QUADS - 1 else nc.sync
-            queue.dma_start(out=out_2[0, 4 * q : 4 * q + 4, :].bitcast(I32), in_=y_plane[32 * q : 32 * q + 4, :].bitcast(I32))
+            nc.sync.dma_start(out=out_2[0, 4 * q : 4 * q + 4, :].bitcast(I32), in_=y_plane[32 * q : 32 * q + 4, :].bitcast(I32))

from contextlib import ExitStack

import concourse.mybir as mybir

K, T, S, V, H, N = 512, 2048, 1024, 512, 512, 512
FLOPS = 2 * K * H * S * 2 + 2 * H * N * V

F32 = mybir.dt.float32
BF16 = mybir.dt.bfloat16
I32 = mybir.dt.int32
U32 = mybir.dt.uint32
U16 = mybir.dt.uint16
U8 = mybir.dt.uint8
FP8X4 = mybir.dt.float8_e4m3fn_x4
FP4X4 = mybir.dt.float4_e2m1fn_x4
MULT = mybir.AluOpType.mult
ADD = mybir.AluOpType.add

P = 128
PACK = 4
QUADS = 4
CHUNK = 128
RECS = CHUNK // 2
GATHER = 256
BLOCK = 128
HALF = H // 2


def load_scale_rows(queue, plane, scales):
    for q in range(QUADS):
        queue.dma_start(out=plane[32 * q : 32 * q + 4, :].bitcast(I32), in_=scales[0, 4 * q : 4 * q + 4, :].bitcast(I32))


def tile_picked_zfm_none_po_kernel(
    tc, x_words, x_scales, w1, w2_words, w2_scales, w3_words, w3_scales, offs, out_0, out_1, out_2
):
    nc = tc.nc
    with ExitStack() as ctx:
        keep = ctx.enter_context(tc.tile_pool(name="keep", bufs=1))
        ring = ctx.enter_context(tc.tile_pool(name="ring", bufs=4))
        psum_e = ctx.enter_context(tc.psum_pool(name="psum_e", bufs=3))
        psum_h = ctx.enter_context(tc.psum_pool(name="psum_h", bufs=3))
        psum_y = ctx.enter_context(tc.psum_pool(name="psum_y", bufs=2))

        offsets = keep.tile([P, S // 16], U16, name="offsets")
        x_table = keep.tile([P, T], U32, name="x_table", align_bytes=64)
        x_table_scales = keep.tile([P, T], U8, name="x_table_scales", align_bytes=64)
        x_plane = keep.tile([P, S], U8, name="x_plane", align_bytes=64)
        w2_raw = keep.tile([P, 2 * H], U8, name="w2_raw", align_bytes=64)
        w3_raw = keep.tile([P, 2 * N], U8, name="w3_raw", align_bytes=64)
        w2_raw_scales = keep.tile([P, H], U8, name="w2_raw_scales", tag="w2_raw_scales", align_bytes=64)
        w3_raw_scales = keep.tile([P, N], U8, name="w3_raw_scales", align_bytes=64)
        w2_codes = keep.tile([P, 2 * H], U8, name="w2_codes", align_bytes=64)
        w3_codes = keep.tile([P, 2 * N], U8, name="w3_codes", align_bytes=64)
        w2_plane = keep.tile([P, H], U8, name="w2_plane", align_bytes=64)
        w1_raw = [keep.tile([P, PACK, HALF], F32, name=f"w1_raw{u}", tag=f"w1_raw{u}", align_bytes=64) for u in range(2)]
        w1_bf = {s: keep.tile([P, 2, P, PACK], BF16, name=f"w1_bf{s}", tag=f"w1_bf{s}", align_bytes=64) for s in (0, 2)}
        w1_codes = keep.tile([P, H], U32, name="w1_codes", align_bytes=64)
        w1_plane = keep.tile([P, H], U8, name="w1_plane", align_bytes=64)
        y_codes = keep.tile([P, V], U32, name="y_codes", align_bytes=64)
        y_plane = keep.tile([P, V], U8, name="y_plane", align_bytes=64)

        nc.vector.memset(w2_raw_scales[:].bitcast(I32), 0)
        nc.vector.memset(w3_raw_scales[:].bitcast(I32), 0)

        for q in range(QUADS):
            queue = nc.sync if q % 2 == 0 else nc.scalar
            queue.dma_start(
                out=x_table_scales[32 * q : 32 * q + 32, :].bitcast(I32),
                in_=x_scales[0, 4 * q : 4 * q + 4, :].bitcast(I32).partition_broadcast(8),
            )
        nc.sync.dma_start(offsets[:], offs)
        nc.sync.dma_start(out=x_table[:].bitcast(I32), in_=x_words[0].rearrange("p n t -> p (n t)").bitcast(I32))
        nc.sync.dma_start(out=w2_raw[:].bitcast(I32), in_=w2_words[0].bitcast(I32))
        load_scale_rows(nc.sync, w2_raw_scales, w2_scales)
        w1_rows = w1.rearrange("(p j) c -> p j c", j=PACK)
        for u in range(2):
            nc.sync.dma_start(out=w1_raw[u][:], in_=w1_rows[:, :, u * HALF : (u + 1) * HALF])
        nc.sync.dma_start(out=w3_raw[:].bitcast(I32), in_=w3_words[0].bitcast(I32))
        load_scale_rows(nc.sync, w3_raw_scales, w3_scales)

        def deal(codes, plane, raw, raw_scales):
            nc.scalar.copy(
                out=codes[:].bitcast(U16).rearrange("p (t m) -> p t m", t=PACK),
                in_=raw[:].bitcast(U16).rearrange("p (m t) -> p t m", t=PACK),
            )
            nc.vector.tensor_copy(
                out=plane[:].rearrange("p (t m) -> p t m", t=PACK),
                in_=raw_scales[:].rearrange("p (m t) -> p t m", t=PACK),
            )

        nc.vector.tensor_copy(x_plane[:], x_table_scales[:].indirect(offsets[:]))
        deal(w2_codes, w2_plane, w2_raw, w2_raw_scales)
        x_parts = {}

        def gather_words(g, codes):
            x_parts[g] = codes
            nc.vector.tensor_copy(codes, x_table[:].indirect(offsets[:, g * GATHER // 16 : (g + 1) * GATHER // 16]))

        x_first = keep.tile([P, GATHER], U32, name="x_first", align_bytes=64)
        gather_words(0, x_first[:])
        x_rest = keep.tile([P, S - GATHER], U32, name="x_rest", tag="w2_raw_scales", align_bytes=64)
        nc.vector.tensor_copy(x_rest[:], x_table[:].indirect(offsets[:, GATHER // 16 :]))
        for g in range(1, S // GATHER):
            x_parts[g] = x_rest[:, (g - 1) * GATHER : g * GATHER]

        def product(bank, lhs_codes, lhs_plane, rhs_codes, rhs_plane, slices=range(PACK)):
            for t in slices:
                nc.tensor.matmul_mx(
                    out=bank[:, t, :],
                    lhsT=lhs_codes(t),
                    lhsT_scale=lhs_plane[:, t * P : (t + 1) * P],
                    rhs=rhs_codes.bitcast(FP8X4),
                    rhs_scale=rhs_plane,
                    start=True,
                    stop=True,
                )

        def w1_slice(t):
            return w1_codes[:, t * P : (t + 1) * P].bitcast(FP8X4)

        def w2_slice(t):
            return w2_codes[:, 2 * t * P : 2 * (t + 1) * P].bitcast(FP4X4)

        def w3_slice(t):
            return w3_codes[:, 2 * t * P : 2 * (t + 1) * P].bitcast(FP4X4)

        def round_w1(u, s, copy):
            m = HALF // PACK
            copy(
                out=w1_bf[s][:, :, u * m : (u + 1) * m, :].rearrange("p t m j -> p m j t"),
                in_=w1_raw[u][:].rearrange("p j (m t) -> p m j t", t=PACK)[:, :, :, s : s + 2],
            )

        def quantize_w1(s):
            cols = slice(s * P, (s + 2) * P)
            nc.vector.quantize_mx(
                out=w1_codes[:, cols].bitcast(FP8X4),
                scales=w1_plane[:, cols],
                in_=w1_bf[s][:].rearrange("p t m j -> p (t m j)"),
            )

        e_sb = {}

        def make_e(c):
            cols = slice(c * CHUNK, (c + 1) * CHUNK)
            e_bank = psum_e.tile([P, PACK, CHUNK], F32, name="e_bank")
            product(e_bank, w2_slice, w2_plane, x_parts[c // 2][:, (c % 2) * CHUNK : (c % 2 + 1) * CHUNK], x_plane[:, cols])
            if c % 4 == 0:
                tag = "w1_raw1" if c == 0 else "e_late"
                e_sb[c // 4] = keep.tile([P, 4, 2, RECS, PACK], F32, name=f"e_sb{c // 4}", tag=tag, align_bytes=64)
            nc.scalar.copy(out=e_sb[c // 4][:, c % 4, :, :, :], in_=e_bank[:].rearrange("p t (v d) -> p d v t", d=2))

        def cross(c, pairs):
            cols = slice(c * CHUNK, (c + 1) * CHUNK)
            h_bank = psum_h.tile([P, PACK, CHUNK], F32, name="h_bank")
            product(h_bank, w1_slice, w1_plane, x_parts[c // 2][:, (c % 2) * CHUNK : (c % 2 + 1) * CHUNK], x_plane[:, cols])
            recs = slice((c % 2) * RECS, (c % 2 + 1) * RECS)
            nc.vector.tensor_tensor(
                out=pairs[:, :, recs, :],
                in0=h_bank[:].rearrange("p t (v d) -> p d v t", d=2),
                in1=e_sb[c // 4][:, c % 4, ::-1, :, :],
                op=MULT,
            )

        round_w1(0, 0, nc.scalar.copy)
        round_w1(0, 2, nc.scalar.copy)
        round_w1(1, 0, nc.scalar.copy)
        round_w1(1, 2, nc.scalar.copy)
        quantize_w1(0)
        quantize_w1(2)
        for c in range(4):
            make_e(c)
        w3_plane = keep.tile([P, N], U8, name="w3_plane", tag="w1_bf2", align_bytes=64)
        deal(w3_codes, w3_plane, w3_raw, w3_raw_scales)

        out_rows = out_0.rearrange("(p t) v -> p t v", t=PACK)
        out_words = out_1[0].rearrange("p v t -> p (v t)").bitcast(I32)
        blocks = V // BLOCK
        z_bf = {}
        y_early = keep.tile([P, V - BLOCK, PACK], BF16, name="y_early", align_bytes=64)
        y_late = keep.tile([P, BLOCK, PACK], BF16, name="y_late", align_bytes=64)

        z_codes = keep.tile([P, V], U32, name="z_codes", align_bytes=64)
        z_plane = keep.tile([P, V], U8, name="z_plane", align_bytes=64)

        def sum_pairs(b, pairs, recs):
            nc.vector.tensor_tensor(
                out=z_bf[b][:, recs, :], in0=pairs[:, 0, recs, :], in1=pairs[:, 1, recs, :], op=ADD
            )

        def quantize_z(b, recs):
            cols = slice(b * BLOCK + recs.start, b * BLOCK + recs.stop)
            nc.vector.quantize_mx(
                out=z_codes[:, cols].bitcast(FP8X4),
                scales=z_plane[:, cols],
                in_=z_bf[b][:, recs, :].rearrange("p v t -> p (v t)"),
            )

        def last_product(b):
            cols = slice(b * BLOCK, (b + 1) * BLOCK)
            y_bank = psum_y.tile([P, PACK, BLOCK], F32, name="y_bank")
            product(y_bank, w3_slice, w3_plane, z_codes[:, cols], z_plane[:, cols])
            nc.scalar.copy(out=y_early[:, cols, :], in_=y_bank[:].rearrange("p t v -> p v t"))
            y_sb = ring.tile([P, PACK, BLOCK], F32, name="y_sb", align_bytes=64)
            nc.scalar.copy(out=y_sb[:], in_=y_bank[:])
            nc.sync.dma_start(out=out_rows[:, :, cols], in_=y_sb[:])

        def last_product_in_two_banks(b):
            cols = slice(b * BLOCK, (b + 1) * BLOCK)
            banks = []
            for s, copy in ((0, nc.scalar.copy), (2, nc.vector.tensor_copy)):
                y_bank = psum_y.tile([P, PACK, BLOCK], F32, name="y_bank")
                banks.append(y_bank)
                product(y_bank, w3_slice, w3_plane, z_codes[:, cols], z_plane[:, cols], range(s, s + 2))
                copy(out=y_late[:, :, s : s + 2], in_=y_bank[:, s : s + 2, :].rearrange("p t v -> p v t"))
            for s in (0, 2):
                y_sb = ring.tile([P, 2, BLOCK], F32, name="y_sb", align_bytes=64)
                nc.scalar.copy(out=y_sb[:], in_=banks[s // 2][:, s : s + 2, :])
                nc.scalar.dma_start(out=out_rows[:, s : s + 2, cols], in_=y_sb[:])

        def hand_on(y_bf, cols):
            nc.vector.quantize_mx(
                out=y_codes[:, cols].bitcast(FP8X4),
                scales=y_plane[:, cols],
                in_=y_bf[:].rearrange("p v t -> p (v t)"),
            )
            nc.sync.dma_start(out=out_words[:, cols], in_=y_codes[:, cols].bitcast(I32))

        whole, first, second = slice(0, BLOCK), slice(0, RECS), slice(RECS, BLOCK)
        pairs = [ring.tile([P, 2, BLOCK, PACK], F32, name="pairs", align_bytes=64) for b in range(blocks)]
        for b in range(blocks):
            z_bf[b] = ring.tile([P, BLOCK, PACK], BF16, name="z_bf", align_bytes=64)
        last = blocks - 1
        cross(0, pairs[0])
        cross(1, pairs[0])
        for b in range(last):
            if 2 * b + 4 < S // CHUNK:
                make_e(2 * b + 4)
                make_e(2 * b + 5)
            cross(2 * b + 2, pairs[b + 1])
            sum_pairs(b, pairs[b], whole)
            if b + 1 == last:
                sum_pairs(last, pairs[last], first)
                quantize_z(b, whole)
                last_product(b)
                cross(2 * b + 3, pairs[b + 1])
            else:
                cross(2 * b + 3, pairs[b + 1])
                quantize_z(b, whole)
                last_product(b)
        quantize_z(last, first)
        sum_pairs(last, pairs[last], second)
        quantize_z(blocks - 1, second)
        hand_on(y_early, slice(0, V - BLOCK))
        last_product_in_two_banks(blocks - 1)
        hand_on(y_late, slice(V - BLOCK, V))
        for q in range(QUADS):
            nc.sync.dma_start(out=out_2[0, 4 * q : 4 * q + 4, :].bitcast(I32), in_=y_plane[32 * q : 32 * q + 4, :].bitcast(I32))
